import numpy as np
import ml_dtypes


def mxq(x, axis, fmt="e4m3"):
    dtype, down = {"e4m3": (ml_dtypes.float8_e4m3fn, 7), "e5m2": (ml_dtypes.float8_e5m2, 14)}[fmt]
    v = np.moveaxis(np.asarray(x, np.float32).astype(ml_dtypes.bfloat16).astype(np.float64), axis, -1)
    blocks = v.reshape(v.shape[:-1] + (-1, 32))
    amax = np.abs(blocks).max(-1, keepdims=True)
    byte = np.maximum(np.where(amax > 0, np.frexp(amax)[1] - 1 + 127, 0) - down, 1)
    scale = np.exp2(byte - 127.0)
    codes = (blocks / scale).astype(np.float32).astype(dtype).astype(np.float64)
    return np.moveaxis((codes * scale).reshape(v.shape), -1, axis)


WIDE = False


def mx_kscale(k):
    if not WIDE:
        return np.ones(k)
    levels = np.array([10, -10, 5, -5, 0])
    if k % 512:
        return np.exp2(np.random.permutation(np.resize(levels, k // 32))).repeat(32)
    a = np.empty((k // 512, 16))
    for p in range(k // 512):
        a[p, :8] = np.random.permutation(np.resize(levels, 8))
        for g in range(8):
            far = levels[np.abs(levels - a[p, g]) >= 10]
            a[p, g + 8] = far[np.random.randint(len(far))]
    return np.exp2(a.ravel()).repeat(32)


def f64(x):
    return np.asarray(x).astype(np.float64)


def striped(idx):
    return np.tile(idx.reshape(-1, 16).T, (8, 1)).astype(np.uint16)


def unstriped(offs):
    return offs[:16].T.reshape(-1).astype(np.int64)


def pack_weight(w):
    k, n = w.shape
    w = f64(np.asarray(w, np.float32).astype(ml_dtypes.bfloat16)).reshape(k // 32, 32, n)
    amax = np.abs(w).max(1)
    byte = np.clip(np.where(amax > 0, np.frexp(amax)[1] - 1 + 127 - 7, 1), 1, 254)
    scaled = (w * np.exp2(127.0 - byte)[:, None, :]).reshape(k, n).astype(np.float32)
    words = np.ascontiguousarray(scaled.reshape(k // 512, 128, 4, n).transpose(0, 1, 3, 2)).astype(ml_dtypes.float8_e4m3fn).view(np.uint8)
    return words, np.ascontiguousarray(byte.astype(np.uint8).reshape(k // 512, 16, n))


def unpack_weight(words, scales):
    g, p, n, _ = words.shape
    vals = np.ascontiguousarray(words).view(ml_dtypes.float8_e4m3fn).astype(np.float64) * np.repeat(np.exp2(scales.astype(np.float64) - 127.0), 8, axis=1)[..., None]
    return vals.transpose(0, 1, 3, 2).reshape(g * 512, n)


K, T, S, V, H, N = 1024, 1024, 512, 256, 512, 128


def setup_inputs():
    n = np.random.standard_normal
    s = mx_kscale(K)[:, None]
    u = mx_kscale(H)
    packed_xT = pack_weight(n((K, T)) * s)
    packed_w2 = pack_weight(n((H, N)) / np.sqrt(3 * H) / u[:, None])
    packed_w3 = pack_weight(n((H, N)) / np.sqrt(3 * H) / u[:, None])
    packed_w4 = pack_weight(n((H, N)) / np.sqrt(3 * H) / u[:, None])
    return {
        "x_words": packed_xT[0],
        "x_scales": packed_xT[1],
        "w1": (n((K, H)) / np.sqrt(K) / s * u).astype(np.float32),
        "w2_words": packed_w2[0],
        "w2_scales": packed_w2[1],
        "w3_words": packed_w3[0],
        "w3_scales": packed_w3[1],
        "w4_words": packed_w4[0],
        "w4_scales": packed_w4[1],
        "offs": striped(np.random.permutation(T)[:S]),
        "pos1": striped(np.random.permutation(S)[:V]),
        "pos2": striped(np.random.permutation(S)[:V]),
        "pos3": striped(np.random.permutation(S)[:V]),
    }


def reference(x_words, x_scales, w1, w2_words, w2_scales, w3_words, w3_scales, w4_words, w4_scales, offs, pos1, pos2, pos3):
    xq = unpack_weight(x_words, x_scales)[:, unstriped(offs)]
    h = mxq(f64(w1), 0, "e4m3").T @ xq
    g0 = h[:, unstriped(pos1)]
    g1 = h[:, unstriped(pos2)]
    g2 = h[:, unstriped(pos3)]
    z1 = (g0 + g1 + g2) / 3
    z2 = np.maximum(np.maximum(g0, g1), g2)
    z3 = np.minimum(np.minimum(g0, g1), g2)
    return unpack_weight(w2_words, w2_scales).T @ mxq(z1, 0, "e4m3") + unpack_weight(w3_words, w3_scales).T @ mxq(z2, 0, "e4m3") + unpack_weight(w4_words, w4_scales).T @ mxq(z3, 0, "e4m3")

@@ -1,0 +1,206 @@
+from contextlib import ExitStack
+
+import concourse.mybir as mybir
+from concourse.masks import make_identity
+
+K, T, S, V, H, N = 1024, 1024, 512, 256, 512, 128
+FLOPS = 2 * K * H * S + 3 * 2 * H * N * V
+
+F32 = mybir.dt.float32
+BF16 = mybir.dt.bfloat16
+I32 = mybir.dt.int32
+U32 = mybir.dt.uint32
+U16 = mybir.dt.uint16
+U8 = mybir.dt.uint8
+FP8X4 = mybir.dt.float8_e4m3fn_x4
+COPY = mybir.ActivationFunctionType.Copy
+MAX = mybir.AluOpType.max
+MIN = mybir.AluOpType.min
+
+P = 128
+PACK = 4
+PASSES = K // (P * PACK)
+SH = S // 2
+VH = V // 2
+
+
+def tile_picked_pna_none_p_kernel(
+    tc, x_words, x_scales, w1, w2_words, w2_scales, w3_words, w3_scales, w4_words, w4_scales, offs, pos1, pos2, pos3, out
+):
+    nc = tc.nc
+    with ExitStack() as ctx:
+        keep = ctx.enter_context(tc.tile_pool(name="keep", bufs=1))
+        psum = ctx.enter_context(tc.psum_pool(name="psum", bufs=1))
+
+        def sb(name, shape, dtype):
+            return keep.tile(shape, dtype, name=name, align_bytes=64)
+
+        def bank(b, shape):
+            return psum.tile(shape, F32, name="bank%d" % b)
+
+        offs_t = sb("offs_t", [P, S // 16], U16)
+        pos_t = [sb("pos_t%d" % d, [P, V // 16], U16) for d in range(3)]
+        xs_all = sb("xs_all", [P, T], U8)
+        ws = sb("ws", [P, 3 * N], U8)
+        xw_all = [sb("xw_all%d" % z, [P, T], U32) for z in range(PASSES)]
+        ww = [sb("ww%d" % d, [P, N], U32) for d in range(3)]
+        ident = sb("ident", [P, P], F32)
+
+        nc.gpsimd.memset(xs_all[:].bitcast(I32), 0)
+        nc.vector.memset(ws[:].bitcast(I32), 0)
+        make_identity(nc, ident[:])
+
+        w1_rows = w1.rearrange("(z p j) c -> z p j c", z=PASSES, j=PACK)
+        chunks = [(0, 0, H), (1, 0, H // 2), (1, H // 2, H)]
+        raw = [sb("raw%d" % n, [P, PACK, c1 - c0], F32) for n, (z, c0, c1) in enumerate(chunks)]
+
+        def load_w1(n):
+            z, c0, c1 = chunks[n]
+            nc.sync.dma_start(out=raw[n][:], in_=w1_rows[z][:, :, c0:c1])
+
+        def load_x(z):
+            nc.sync.dma_start(out=xw_all[z][:].bitcast(I32), in_=x_words[z].rearrange("p c r -> p (c r)").bitcast(I32))
+
+        nc.sync.dma_start(offs_t[:], offs)
+        load_w1(0)
+        for q in range(4):
+            nc.sync.dma_start(
+                out=xs_all[32 * q : 32 * q + 4 * PASSES, :].bitcast(I32), in_=x_scales[:, 4 * q : 4 * q + 4, :].bitcast(I32)
+            )
+        load_x(0)
+        load_w1(1)
+        load_w1(2)
+        load_x(1)
+        for d, pos in enumerate((pos1, pos2, pos3)):
+            nc.sync.dma_start(pos_t[d][:], pos)
+        for d, (words, scales) in enumerate(((w2_words, w2_scales), (w3_words, w3_scales), (w4_words, w4_scales))):
+            nc.sync.dma_start(out=ww[d][:].bitcast(I32), in_=words[0].rearrange("p c r -> p (c r)").bitcast(I32))
+            for q in range(4):
+                nc.sync.dma_start(
+                    out=ws[32 * q : 32 * q + 4, d * N : (d + 1) * N].bitcast(I32), in_=scales[0][4 * q : 4 * q + 4, :].bitcast(I32)
+                )
+
+        w1b = [sb("w1b%d" % z, [P, PACK, P, PACK], BF16) for z in range(PASSES)]
+        w1c = [sb("w1c%d" % z, [P, H], U32) for z in range(PASSES)]
+        w1s = [sb("w1s%d" % z, [P, H], U8) for z in range(PASSES)]
+        xs = sb("xs", [P, S], U8)
+        xw = [[sb("xw%d_%d" % (z, a), [P, SH], U32) for a in range(2)] for z in range(PASSES)]
+
+        def cast_w1(n, m0, m1, on_vector):
+            z, c0, c1 = chunks[n]
+            src = raw[n][:].rearrange("p j (m t) -> p m j t", t=PACK)[:, m0:m1]
+            dst = w1b[z][:].rearrange("p t m j -> p m j t")[:, c0 // PACK + m0 : c0 // PACK + m1]
+            if on_vector:
+                nc.vector.tensor_copy(out=dst, in_=src)
+            else:
+                nc.scalar.copy(out=dst, in_=src)
+
+        def quant_w1(z):
+            nc.vector.quantize_mx(out=w1c[z][:].bitcast(FP8X4), scales=w1s[z][:], in_=w1b[z][:].rearrange("p t m j -> p (t m j)"))
+
+        def gather_x(z, a):
+            nc.vector.tensor_copy(xw[z][a][:], xw_all[z][:].indirect(offs_t[:, a * SH // 16 : (a + 1) * SH // 16]))
+
+        nc.vector.tensor_copy(xs[:], xs_all[:].indirect(offs_t[:]))
+        cast_w1(0, 0, 64, True)
+        cast_w1(0, 64, 128, False)
+        gather_x(0, 0)
+        gather_x(0, 1)
+        quant_w1(0)
+        cast_w1(1, 0, 64, False)
+        cast_w1(2, 0, 44, True)
+        cast_w1(2, 44, 64, False)
+        quant_w1(1)
+        gather_x(1, 0)
+        gather_x(1, 1)
+
+        hp = [[bank(2 * t + a, [P, SH]) for a in range(2)] for t in range(PACK)]
+        h = [sb("h%d" % t, [P, S], F32) for t in range(PACK)]
+
+        def first_product(z, t, a):
+            nc.tensor.matmul_mx(
+                out=hp[t][a][:],
+                lhsT=w1c[z][:, t * P : (t + 1) * P].bitcast(FP8X4),
+                lhsT_scale=w1s[z][:, t * P : (t + 1) * P],
+                rhs=xw[z][a][:].bitcast(FP8X4),
+                rhs_scale=xs[4 * z :, a * SH : (a + 1) * SH],
+                start=(z == 0),
+                stop=(z == PASSES - 1),
+            )
+
+        for a in range(2):
+            for t in range(PACK):
+                first_product(0, t, a)
+        for t, a in ((0, 0), (1, 0), (0, 1), (1, 1), (2, 0), (2, 1), (3, 0), (3, 1)):
+            first_product(1, t, a)
+        for t in range(PACK):
+            for a in range(2):
+                nc.scalar.copy(out=h[t][:, a * SH : (a + 1) * SH], in_=hp[t][a][:])
+
+        g = [sb("g%d" % d, [P, PACK, V], F32) for d in range(2)]
+        gb = [sb("gb%d" % d, [P, V, PACK], BF16) for d in range(2)]
+        g2 = [sb("g2_%d" % a, [P, PACK, VH], F32) for a in range(2)]
+        g2b = sb("g2b", [P, V, PACK], BF16)
+        hi = sb("hi", [P, V * PACK], BF16)
+        lo = sb("lo", [P, V * PACK], BF16)
+
+        def cast_g(dst, src):
+            nc.scalar.copy(out=dst.rearrange("p (c i) t -> p c t i", i=4), in_=src.rearrange("p t (c i) -> p c t i", i=4))
+
+        for d in range(2):
+            for t in range(PACK):
+                nc.vector.tensor_copy(g[d][:, t, :], h[t][:].indirect(pos_t[d][:]))
+            cast_g(gb[d][:], g[d][:])
+        flat = [gb[d][:].rearrange("p v t -> p (v t)") for d in range(2)]
+        nc.vector.tensor_tensor(hi[:], flat[0], flat[1], MAX)
+        nc.vector.tensor_tensor(lo[:], flat[0], flat[1], MIN)
+        for a in range(2):
+            for t in range(PACK):
+                nc.vector.tensor_copy(g2[a][:, t, :], h[t][:].indirect(pos_t[2][:, a * VH // 16 : (a + 1) * VH // 16]))
+
+        z = [sb("z%d" % d, [P, V * PACK], BF16) for d in range(3)]
+        for a in range(2):
+            cols = slice(a * VH, (a + 1) * VH)
+            cast_g(g2b[:, cols, :], g2[a][:])
+            total = bank(a, [P, PACK, P])
+            for t in range(PACK):
+                for d, src in enumerate((g[0][:, t, cols], g[1][:, t, cols], g2[a][:, t, :])):
+                    nc.tensor.matmul(total[:, t, :], src, ident[:], start=(d == 0), stop=(d == 2), is_transpose=True)
+            mean_t = sb("mean_t%d" % a, [P, 2, P, 2], BF16)
+            nc.scalar.activation(mean_t[:], total[:].rearrange("v (u e) p -> v u p e", e=2), COPY, scale=1.0 / 3.0)
+            back = bank(2 + a, [P, 2, P])
+            pairs = mean_t[:].rearrange("v u p e -> v (u p e)").bitcast(F32)
+            for u in range(2):
+                nc.tensor.transpose(back[:, u, :], pairs[:, u * P : (u + 1) * P], ident[:])
+            z_pairs = z[0][:].bitcast(F32)[:, a * VH * 2 : (a + 1) * VH * 2]
+            nc.scalar.copy(out=z_pairs.rearrange("p (v u) -> p v u", u=2), in_=back[:].rearrange("p u v -> p v u"))
+
+        third = g2b[:].rearrange("p v t -> p (v t)")
+        nc.vector.tensor_tensor(z[1][:], hi[:], third, MAX)
+        nc.vector.tensor_tensor(z[2][:], lo[:], third, MIN)
+        zc = [sb("zc%d" % d, [P, V], U32) for d in range(3)]
+        zs = [sb("zs%d" % d, [P, V], U8) for d in range(3)]
+        for d in (1, 0):
+            nc.vector.quantize_mx(out=zc[d][:].bitcast(FP8X4), scales=zs[d][:], in_=z[d][:])
+        for a in range(2):
+            cols = slice(a * VH, (a + 1) * VH)
+            nc.vector.quantize_mx(out=zc[2][:, cols].bitcast(FP8X4), scales=zs[2][:, cols], in_=z[2][:, a * VH * PACK : (a + 1) * VH * PACK])
+
+        acc = [bank(4 + a, [P, VH]) for a in range(2)]
+        for n, d in enumerate((1, 0, 2)):
+            for a in range(2):
+                cols = slice(a * VH, (a + 1) * VH)
+                nc.tensor.matmul_mx(
+                    out=acc[a][:],
+                    lhsT=ww[d][:].bitcast(FP8X4),
+                    lhsT_scale=ws[:, d * N : (d + 1) * N],
+                    rhs=zc[d][:, cols].bitcast(FP8X4),
+                    rhs_scale=zs[d][:, cols],
+                    start=(n == 0),
+                    stop=(n == 2),
+                )
+        for a in range(2):
+            cols = slice(a * VH, (a + 1) * VH)
+            res = sb("res%d" % a, [P, VH], F32)
+            nc.scalar.copy(out=res[:], in_=acc[a][:])
+            nc.sync.dma_start(out=out[:, cols], in_=res[:])

@@ -101,9 +101,9 @@ def tile_picked_pna_none_p_kernel(
         def gather_x(z, a):
             nc.vector.tensor_copy(xw[z][a][:], xw_all[z][:].indirect(offs_t[:, a * SH // 16 : (a + 1) * SH // 16]))
 
+        cast_w1(0, 0, 32, True)
+        cast_w1(0, 32, 128, False)
         nc.vector.tensor_copy(xs[:], xs_all[:].indirect(offs_t[:]))
-        cast_w1(0, 0, 64, True)
-        cast_w1(0, 64, 128, False)
         gather_x(0, 0)
         gather_x(0, 1)
         quant_w1(0)
@@ -115,7 +115,7 @@ def tile_picked_pna_none_p_kernel(
         gather_x(1, 1)
 
         hp = [[bank(2 * t + a, [P, SH]) for a in range(2)] for t in range(PACK)]
-        h = [sb("h%d" % t, [P, S], F32) for t in range(PACK)]
+        h = sb("h", [P, PACK * S], F32)
 
         def first_product(z, t, a):
             nc.tensor.matmul_mx(
@@ -135,59 +135,53 @@ def tile_picked_pna_none_p_kernel(
             first_product(1, t, a)
         for t in range(PACK):
             for a in range(2):
-                nc.scalar.copy(out=h[t][:, a * SH : (a + 1) * SH], in_=hp[t][a][:])
+                nc.scalar.copy(out=h[:, t * S + a * SH : t * S + (a + 1) * SH], in_=hp[t][a][:])
 
-        g = [sb("g%d" % d, [P, PACK, V], F32) for d in range(2)]
-        gb = [sb("gb%d" % d, [P, V, PACK], BF16) for d in range(2)]
-        g2 = [sb("g2_%d" % a, [P, PACK, VH], F32) for a in range(2)]
-        g2b = sb("g2b", [P, V, PACK], BF16)
+        g = [sb("g%d" % d, [P, PACK, V], F32) for d in range(3)]
+        gb = [sb("gb%d" % d, [P, V, PACK], BF16) for d in range(3)]
         hi = sb("hi", [P, V * PACK], BF16)
         lo = sb("lo", [P, V * PACK], BF16)
 
-        def cast_g(dst, src):
-            nc.scalar.copy(out=dst.rearrange("p (c i) t -> p c t i", i=4), in_=src.rearrange("p t (c i) -> p c t i", i=4))
-
-        for d in range(2):
+        for d in range(3):
             for t in range(PACK):
-                nc.vector.tensor_copy(g[d][:, t, :], h[t][:].indirect(pos_t[d][:]))
-            cast_g(gb[d][:], g[d][:])
-        flat = [gb[d][:].rearrange("p v t -> p (v t)") for d in range(2)]
+                end = (t + 1) * S if d == 0 else PACK * S
+                nc.vector.tensor_copy(g[d][:, t, :], h[:, t * S : end].indirect(pos_t[d][:]))
+            nc.scalar.copy(out=gb[d][:].rearrange("p (c i) t -> p c t i", i=4), in_=g[d][:].rearrange("p t (c i) -> p c t i", i=4))
+        flat = [gb[d][:].rearrange("p v t -> p (v t)") for d in range(3)]
         nc.vector.tensor_tensor(hi[:], flat[0], flat[1], MAX)
         nc.vector.tensor_tensor(lo[:], flat[0], flat[1], MIN)
-        for a in range(2):
-            for t in range(PACK):
-                nc.vector.tensor_copy(g2[a][:, t, :], h[t][:].indirect(pos_t[2][:, a * VH // 16 : (a + 1) * VH // 16]))
 
         z = [sb("z%d" % d, [P, V * PACK], BF16) for d in range(3)]
+        total = [bank(a, [P, PACK, P]) for a in range(2)]
+        for t in range(PACK):
+            for a in range(2):
+                for d in range(3):
+                    nc.tensor.matmul(
+                        total[a][:, t, :], g[d][:, t, a * VH : (a + 1) * VH], ident[:], start=(d == 0), stop=(d == 2), is_transpose=True
+                    )
+        back = [bank(2 + a, [P, 2, P]) for a in range(2)]
         for a in range(2):
-            cols = slice(a * VH, (a + 1) * VH)
-            cast_g(g2b[:, cols, :], g2[a][:])
-            total = bank(a, [P, PACK, P])
-            for t in range(PACK):
-                for d, src in enumerate((g[0][:, t, cols], g[1][:, t, cols], g2[a][:, t, :])):
-                    nc.tensor.matmul(total[:, t, :], src, ident[:], start=(d == 0), stop=(d == 2), is_transpose=True)
             mean_t = sb("mean_t%d" % a, [P, 2, P, 2], BF16)
-            nc.scalar.activation(mean_t[:], total[:].rearrange("v (u e) p -> v u p e", e=2), COPY, scale=1.0 / 3.0)
-            back = bank(2 + a, [P, 2, P])
+            nc.scalar.activation(mean_t[:], total[a][:].rearrange("v (u e) p -> v u p e", e=2), COPY, scale=1.0 / 3.0)
             pairs = mean_t[:].rearrange("v u p e -> v (u p e)").bitcast(F32)
             for u in range(2):
-                nc.tensor.transpose(back[:, u, :], pairs[:, u * P : (u + 1) * P], ident[:])
+                nc.tensor.transpose(back[a][:, u, :], pairs[:, u * P : (u + 1) * P], ident[:])
+        for a in range(2):
             z_pairs = z[0][:].bitcast(F32)[:, a * VH * 2 : (a + 1) * VH * 2]
-            nc.scalar.copy(out=z_pairs.rearrange("p (v u) -> p v u", u=2), in_=back[:].rearrange("p u v -> p v u"))
+            nc.scalar.copy(out=z_pairs.rearrange("p (v u) -> p v u", u=2), in_=back[a][:].rearrange("p u v -> p v u"))
 
-        third = g2b[:].rearrange("p v t -> p (v t)")
-        nc.vector.tensor_tensor(z[1][:], hi[:], third, MAX)
-        nc.vector.tensor_tensor(z[2][:], lo[:], third, MIN)
+        nc.vector.tensor_tensor(z[1][:], hi[:], flat[2], MAX)
+        nc.vector.tensor_tensor(z[2][:], lo[:], flat[2], MIN)
         zc = [sb("zc%d" % d, [P, V], U32) for d in range(3)]
         zs = [sb("zs%d" % d, [P, V], U8) for d in range(3)]
-        for d in (1, 0):
+        for d in (1, 2):
             nc.vector.quantize_mx(out=zc[d][:].bitcast(FP8X4), scales=zs[d][:], in_=z[d][:])
         for a in range(2):
             cols = slice(a * VH, (a + 1) * VH)
-            nc.vector.quantize_mx(out=zc[2][:, cols].bitcast(FP8X4), scales=zs[2][:, cols], in_=z[2][:, a * VH * PACK : (a + 1) * VH * PACK])
+            nc.vector.quantize_mx(out=zc[0][:, cols].bitcast(FP8X4), scales=zs[0][:, cols], in_=z[0][:, a * VH * PACK : (a + 1) * VH * PACK])
 
         acc = [bank(4 + a, [P, VH]) for a in range(2)]
-        for n, d in enumerate((1, 0, 2)):
+        for n, d in enumerate((1, 2, 0)):
             for a in range(2):
                 cols = slice(a * VH, (a + 1) * VH)
                 nc.tensor.matmul_mx(

@@ -51,7 +51,7 @@ def tile_picked_pna_none_p_kernel(
         make_identity(nc, ident[:])
 
         w1_rows = w1.rearrange("(z p j) c -> z p j c", z=PASSES, j=PACK)
-        chunks = [(0, 0, H), (1, 0, H // 2), (1, H // 2, H)]
+        chunks = [(0, 0, 256), (0, 256, 512), (1, 0, 256), (1, 256, 384), (1, 384, 512)]
         raw = [sb("raw%d" % n, [P, PACK, c1 - c0], F32) for n, (z, c0, c1) in enumerate(chunks)]
 
         def load_w1(n):
@@ -61,16 +61,17 @@ def tile_picked_pna_none_p_kernel(
         def load_x(z):
             nc.sync.dma_start(out=xw_all[z][:].bitcast(I32), in_=x_words[z].rearrange("p c r -> p (c r)").bitcast(I32))
 
-        nc.sync.dma_start(offs_t[:], offs)
         load_w1(0)
+        nc.sync.dma_start(offs_t[:], offs)
         for q in range(4):
             nc.sync.dma_start(
                 out=xs_all[32 * q : 32 * q + 4 * PASSES, :].bitcast(I32), in_=x_scales[:, 4 * q : 4 * q + 4, :].bitcast(I32)
             )
         load_x(0)
         load_w1(1)
-        load_w1(2)
         load_x(1)
+        for n in (2, 3, 4):
+            load_w1(n)
         for d, pos in enumerate((pos1, pos2, pos3)):
             nc.sync.dma_start(pos_t[d][:], pos)
         for d, (words, scales) in enumerate(((w2_words, w2_scales), (w3_words, w3_scales), (w4_words, w4_scales))):
@@ -95,24 +96,33 @@ def tile_picked_pna_none_p_kernel(
             else:
                 nc.scalar.copy(out=dst, in_=src)
 
-        def quant_w1(z):
-            nc.vector.quantize_mx(out=w1c[z][:].bitcast(FP8X4), scales=w1s[z][:], in_=w1b[z][:].rearrange("p t m j -> p (t m j)"))
+        def quant_w1(z, t0, t1):
+            nc.vector.quantize_mx(
+                out=w1c[z][:, t0 * P : t1 * P].bitcast(FP8X4),
+                scales=w1s[z][:, t0 * P : t1 * P],
+                in_=w1b[z][:, t0:t1].rearrange("p t m j -> p (t m j)"),
+            )
 
         def gather_x(z, a):
             nc.vector.tensor_copy(xw[z][a][:], xw_all[z][:].indirect(offs_t[:, a * SH // 16 : (a + 1) * SH // 16]))
 
-        cast_w1(0, 0, 32, True)
-        cast_w1(0, 32, 128, False)
         nc.vector.tensor_copy(xs[:], xs_all[:].indirect(offs_t[:]))
+        cast_w1(0, 0, 64, False)
         gather_x(0, 0)
         gather_x(0, 1)
-        quant_w1(0)
-        cast_w1(1, 0, 64, False)
-        cast_w1(2, 0, 44, True)
-        cast_w1(2, 44, 64, False)
-        quant_w1(1)
+        cast_w1(1, 0, 32, False)
+        cast_w1(1, 32, 64, True)
+        quant_w1(0, 0, 4)
         gather_x(1, 0)
         gather_x(1, 1)
+        cast_w1(2, 0, 48, False)
+        cast_w1(2, 48, 64, True)
+        cast_w1(3, 0, 32, True)
+        cast_w1(4, 0, 20, True)
+        cast_w1(4, 20, 32, False)
+        quant_w1(1, 0, 1)
+        quant_w1(1, 1, 2)
+        quant_w1(1, 2, 4)
 
         hp = [[bank(2 * t + a, [P, SH]) for a in range(2)] for t in range(PACK)]
         h = sb("h", [P, PACK * S], F32)
@@ -128,14 +138,17 @@ def tile_picked_pna_none_p_kernel(
                 stop=(z == PASSES - 1),
             )
 
-        for a in range(2):
+        for z in range(PASSES):
             for t in range(PACK):
-                first_product(0, t, a)
-        for t, a in ((0, 0), (1, 0), (0, 1), (1, 1), (2, 0), (2, 1), (3, 0), (3, 1)):
-            first_product(1, t, a)
+                for a in range(2):
+                    first_product(z, t, a)
         for t in range(PACK):
             for a in range(2):
-                nc.scalar.copy(out=h[:, t * S + a * SH : t * S + (a + 1) * SH], in_=hp[t][a][:])
+                dst = h[:, t * S + a * SH : t * S + (a + 1) * SH]
+                if (t, a) == (0, 1):
+                    nc.vector.tensor_copy(out=dst, in_=hp[t][a][:])
+                else:
+                    nc.scalar.copy(out=dst, in_=hp[t][a][:])
 
         g = [sb("g%d" % d, [P, PACK, V], F32) for d in range(3)]
         gb = [sb("gb%d" % d, [P, V, PACK], BF16) for d in range(3)]

@@ -85,7 +85,7 @@ def tile_picked_pna_none_p_kernel(
         w1c = [sb("w1c%d" % z, [P, H], U32) for z in range(PASSES)]
         w1s = [sb("w1s%d" % z, [P, H], U8) for z in range(PASSES)]
         xs = sb("xs", [P, S], U8)
-        xw = [[sb("xw%d_%d" % (z, a), [P, SH], U32) for a in range(2)] for z in range(PASSES)]
+        xw = [sb("xw%d" % z, [P, S], U32) for z in range(PASSES)]
 
         def cast_w1(n, m0, m1, on_vector):
             z, c0, c1 = chunks[n]
@@ -103,18 +103,18 @@ def tile_picked_pna_none_p_kernel(
                 in_=w1b[z][:, t0:t1].rearrange("p t m j -> p (t m j)"),
             )
 
-        def gather_x(z, a):
-            nc.vector.tensor_copy(xw[z][a][:], xw_all[z][:].indirect(offs_t[:, a * SH // 16 : (a + 1) * SH // 16]))
+        def gather_x(z):
+            nc.vector.tensor_copy(xw[z][:], xw_all[z][:].indirect(offs_t[:]))
 
         nc.vector.tensor_copy(xs[:], xs_all[:].indirect(offs_t[:]))
         cast_w1(0, 0, 64, False)
-        gather_x(0, 0)
-        gather_x(0, 1)
+        gather_x(0)
         cast_w1(1, 0, 32, False)
         cast_w1(1, 32, 64, True)
-        quant_w1(0, 0, 4)
-        gather_x(1, 0)
-        gather_x(1, 1)
+        quant_w1(0, 0, 1)
+        quant_w1(0, 1, 2)
+        quant_w1(0, 2, 4)
+        gather_x(1)
         cast_w1(2, 0, 48, False)
         cast_w1(2, 48, 64, True)
         cast_w1(3, 0, 32, True)
@@ -132,7 +132,7 @@ def tile_picked_pna_none_p_kernel(
                 out=hp[t][a][:],
                 lhsT=w1c[z][:, t * P : (t + 1) * P].bitcast(FP8X4),
                 lhsT_scale=w1s[z][:, t * P : (t + 1) * P],
-                rhs=xw[z][a][:].bitcast(FP8X4),
+                rhs=xw[z][:, a * SH : (a + 1) * SH].bitcast(FP8X4),
                 rhs_scale=xs[4 * z :, a * SH : (a + 1) * SH],
                 start=(z == 0),
                 stop=(z == PASSES - 1),
@@ -145,46 +145,60 @@ def tile_picked_pna_none_p_kernel(
         for t in range(PACK):
             for a in range(2):
                 dst = h[:, t * S + a * SH : t * S + (a + 1) * SH]
-                if (t, a) == (0, 1):
+                if (t, a) == (0, 0):
                     nc.vector.tensor_copy(out=dst, in_=hp[t][a][:])
                 else:
                     nc.scalar.copy(out=dst, in_=hp[t][a][:])
 
         g = [sb("g%d" % d, [P, PACK, V], F32) for d in range(3)]
-        gb = [sb("gb%d" % d, [P, V, PACK], BF16) for d in range(3)]
+        gb = [sb("gb%d" % d, [P, V, PACK], BF16) for d in range(2)]
+        last = sb("last", [P, 2, V, 2], BF16)
         hi = sb("hi", [P, V * PACK], BF16)
         lo = sb("lo", [P, V * PACK], BF16)
+        z = [sb("z%d" % d, [P, V * PACK], BF16) for d in range(3)]
+        total = [bank(u, [P, 2, 2, P]) for u in range(2)]
+        back = [bank(2 + a, [P, 2, P]) for a in range(2)]
 
         for d in range(3):
             for t in range(PACK):
                 end = (t + 1) * S if d == 0 else PACK * S
                 nc.vector.tensor_copy(g[d][:, t, :], h[:, t * S : end].indirect(pos_t[d][:]))
-            nc.scalar.copy(out=gb[d][:].rearrange("p (c i) t -> p c t i", i=4), in_=g[d][:].rearrange("p t (c i) -> p c t i", i=4))
-        flat = [gb[d][:].rearrange("p v t -> p (v t)") for d in range(3)]
-        nc.vector.tensor_tensor(hi[:], flat[0], flat[1], MAX)
-        nc.vector.tensor_tensor(lo[:], flat[0], flat[1], MIN)
-
-        z = [sb("z%d" % d, [P, V * PACK], BF16) for d in range(3)]
-        total = [bank(a, [P, PACK, P]) for a in range(2)]
-        for t in range(PACK):
-            for a in range(2):
-                for d in range(3):
+                u, e = divmod(t, 2)
+                for a in range(2):
                     nc.tensor.matmul(
-                        total[a][:, t, :], g[d][:, t, a * VH : (a + 1) * VH], ident[:], start=(d == 0), stop=(d == 2), is_transpose=True
+                        total[u][:, a, e, :],
+                        g[d][:, t, a * VH : (a + 1) * VH],
+                        ident[:],
+                        start=((d, e, a) == (0, 0, 0)),
+                        stop=((d, e, a) == (2, 1, 1)),
+                        is_transpose=True,
                     )
-        back = [bank(2 + a, [P, 2, P]) for a in range(2)]
-        for a in range(2):
-            mean_t = sb("mean_t%d" % a, [P, 2, P, 2], BF16)
-            nc.scalar.activation(mean_t[:], total[a][:].rearrange("v (u e) p -> v u p e", e=2), COPY, scale=1.0 / 3.0)
-            pairs = mean_t[:].rearrange("v u p e -> v (u p e)").bitcast(F32)
-            for u in range(2):
-                nc.tensor.transpose(back[a][:, u, :], pairs[:, u * P : (u + 1) * P], ident[:])
+            if d < 2:
+                nc.scalar.copy(out=gb[d][:].rearrange("p (c i) t -> p c t i", i=4), in_=g[d][:].rearrange("p t (c i) -> p c t i", i=4))
+        for u in range(2):
+            nc.scalar.copy(
+                out=last[:, u].rearrange("p (c i) e -> p c e i", i=4),
+                in_=g[2][:, 2 * u : 2 * u + 2, :].rearrange("p e (c i) -> p c e i", i=4),
+            )
+            mean_t = sb("mean_t%d" % u, [P, 2, P, 2], BF16)
+            nc.scalar.activation(mean_t[:], total[u][:].rearrange("v a e p -> v a p e"), COPY, scale=1.0 / 3.0)
+            pairs = mean_t[:].rearrange("v a p e -> v (a p e)").bitcast(F32)
+            for a in range(2):
+                nc.tensor.transpose(back[a][:, u, :], pairs[:, a * P : (a + 1) * P], ident[:])
         for a in range(2):
             z_pairs = z[0][:].bitcast(F32)[:, a * VH * 2 : (a + 1) * VH * 2]
             nc.scalar.copy(out=z_pairs.rearrange("p (v u) -> p v u", u=2), in_=back[a][:].rearrange("p u v -> p v u"))
 
-        nc.vector.tensor_tensor(z[1][:], hi[:], flat[2], MAX)
-        nc.vector.tensor_tensor(z[2][:], lo[:], flat[2], MIN)
+        flat = [gb[d][:].rearrange("p v t -> p (v t)") for d in range(2)]
+        nc.vector.tensor_tensor(hi[:], flat[0], flat[1], MAX)
+        nc.vector.tensor_tensor(lo[:], flat[0], flat[1], MIN)
+
+        def by_pairs(tile):
+            return tile[:].rearrange("p (v u e) -> p v u e", u=2, e=2)
+
+        last_v = last[:].rearrange("p u v e -> p v u e")
+        nc.vector.tensor_tensor(by_pairs(z[1]), by_pairs(hi), last_v, MAX)
+        nc.vector.tensor_tensor(by_pairs(z[2]), by_pairs(lo), last_v, MIN)
         zc = [sb("zc%d" % d, [P, V], U32) for d in range(3)]
         zs = [sb("zs%d" % d, [P, V], U8) for d in range(3)]
         for d in (1, 2):
@@ -210,4 +224,4 @@ def tile_picked_pna_none_p_kernel(
             cols = slice(a * VH, (a + 1) * VH)
             res = sb("res%d" % a, [P, VH], F32)
             nc.scalar.copy(out=res[:], in_=acc[a][:])
-            nc.sync.dma_start(out=out[:, cols], in_=res[:])
+            (nc.sync, nc.scalar)[a].dma_start(out=out[:, cols], in_=res[:])

@@ -32,8 +32,8 @@ def tile_picked_pna_none_p_kernel(
         keep = ctx.enter_context(tc.tile_pool(name="keep", bufs=1))
         psum = ctx.enter_context(tc.psum_pool(name="psum", bufs=1))
 
-        def sb(name, shape, dtype):
-            return keep.tile(shape, dtype, name=name, align_bytes=64)
+        def sb(name, shape, dtype, tag=""):
+            return keep.tile(shape, dtype, name=name, tag=tag or name, align_bytes=64)
 
         def bank(b, shape):
             return psum.tile(shape, F32, name="bank%d" % b)
@@ -48,7 +48,6 @@ def tile_picked_pna_none_p_kernel(
 
         nc.gpsimd.memset(xs_all[:].bitcast(I32), 0)
         nc.vector.memset(ws[:].bitcast(I32), 0)
-        make_identity(nc, ident[:])
 
         w1_rows = w1.rearrange("(z p j) c -> z p j c", z=PASSES, j=PACK)
         chunks = [(0, 0, 256), (0, 256, 512), (1, 0, 256), (1, 256, 384), (1, 384, 512)]
@@ -61,13 +60,14 @@ def tile_picked_pna_none_p_kernel(
         def load_x(z):
             nc.sync.dma_start(out=xw_all[z][:].bitcast(I32), in_=x_words[z].rearrange("p c r -> p (c r)").bitcast(I32))
 
-        load_w1(0)
+        load_x(0)
         nc.sync.dma_start(offs_t[:], offs)
         for q in range(4):
             nc.sync.dma_start(
                 out=xs_all[32 * q : 32 * q + 4 * PASSES, :].bitcast(I32), in_=x_scales[:, 4 * q : 4 * q + 4, :].bitcast(I32)
             )
-        load_x(0)
+        make_identity(nc, ident[:])
+        load_w1(0)
         load_w1(1)
         load_x(1)
         for n in (2, 3, 4):
@@ -85,7 +85,7 @@ def tile_picked_pna_none_p_kernel(
         w1c = [sb("w1c%d" % z, [P, H], U32) for z in range(PASSES)]
         w1s = [sb("w1s%d" % z, [P, H], U8) for z in range(PASSES)]
         xs = sb("xs", [P, S], U8)
-        xw = [sb("xw%d" % z, [P, S], U32) for z in range(PASSES)]
+        xw = []
 
         def cast_w1(n, m0, m1, on_vector):
             z, c0, c1 = chunks[n]
@@ -103,23 +103,23 @@ def tile_picked_pna_none_p_kernel(
                 in_=w1b[z][:, t0:t1].rearrange("p t m j -> p (t m j)"),
             )
 
-        def gather_x(z):
+        def gather_x(z, tag):
+            xw.append(sb("xw%d" % z, [P, S], U32, tag))
             nc.vector.tensor_copy(xw[z][:], xw_all[z][:].indirect(offs_t[:]))
 
+        gather_x(0, "xw0")
         nc.vector.tensor_copy(xs[:], xs_all[:].indirect(offs_t[:]))
         cast_w1(0, 0, 64, False)
-        gather_x(0)
         cast_w1(1, 0, 32, False)
         cast_w1(1, 32, 64, True)
         quant_w1(0, 0, 1)
         quant_w1(0, 1, 2)
         quant_w1(0, 2, 4)
-        gather_x(1)
-        cast_w1(2, 0, 48, False)
-        cast_w1(2, 48, 64, True)
+        gather_x(1, "w1b0")
+        cast_w1(2, 0, 64, False)
         cast_w1(3, 0, 32, True)
-        cast_w1(4, 0, 20, True)
-        cast_w1(4, 20, 32, False)
+        cast_w1(4, 0, 16, True)
+        cast_w1(4, 16, 32, False)
         quant_w1(1, 0, 1)
         quant_w1(1, 1, 2)
         quant_w1(1, 2, 4)
@@ -150,55 +150,47 @@ def tile_picked_pna_none_p_kernel(
                 else:
                     nc.scalar.copy(out=dst, in_=hp[t][a][:])
 
-        g = [sb("g%d" % d, [P, PACK, V], F32) for d in range(3)]
-        gb = [sb("gb%d" % d, [P, V, PACK], BF16) for d in range(2)]
-        last = sb("last", [P, 2, V, 2], BF16)
+        gb = [sb("gb%d" % d, [P, V, PACK], BF16) for d in range(3)]
         hi = sb("hi", [P, V * PACK], BF16)
         lo = sb("lo", [P, V * PACK], BF16)
         z = [sb("z%d" % d, [P, V * PACK], BF16) for d in range(3)]
-        total = [bank(u, [P, 2, 2, P]) for u in range(2)]
+        total = [bank(a, [P, PACK, P]) for a in range(2)]
         back = [bank(2 + a, [P, 2, P]) for a in range(2)]
 
-        for d in range(3):
+        def round_planes(dst, src):
+            nc.scalar.copy(out=dst.rearrange("p (c i) t -> p c t i", i=4), in_=src.rearrange("p t (c i) -> p c t i", i=4))
+
+        def add_to_total(d, t, a, src):
+            nc.tensor.matmul(total[a][:, t, :], src, ident[:], start=((d, t) == (0, 0)), stop=((d, t) == (2, PACK - 1)), is_transpose=True)
+
+        for d in range(2):
+            g = sb("g%d" % d, [P, PACK, V], F32)
             for t in range(PACK):
                 end = (t + 1) * S if d == 0 else PACK * S
-                nc.vector.tensor_copy(g[d][:, t, :], h[:, t * S : end].indirect(pos_t[d][:]))
-                u, e = divmod(t, 2)
+                nc.vector.tensor_copy(g[:, t, :], h[:, t * S : end].indirect(pos_t[d][:]))
                 for a in range(2):
-                    nc.tensor.matmul(
-                        total[u][:, a, e, :],
-                        g[d][:, t, a * VH : (a + 1) * VH],
-                        ident[:],
-                        start=((d, e, a) == (0, 0, 0)),
-                        stop=((d, e, a) == (2, 1, 1)),
-                        is_transpose=True,
-                    )
-            if d < 2:
-                nc.scalar.copy(out=gb[d][:].rearrange("p (c i) t -> p c t i", i=4), in_=g[d][:].rearrange("p t (c i) -> p c t i", i=4))
-        for u in range(2):
-            nc.scalar.copy(
-                out=last[:, u].rearrange("p (c i) e -> p c e i", i=4),
-                in_=g[2][:, 2 * u : 2 * u + 2, :].rearrange("p e (c i) -> p c e i", i=4),
-            )
-            mean_t = sb("mean_t%d" % u, [P, 2, P, 2], BF16)
-            nc.scalar.activation(mean_t[:], total[u][:].rearrange("v a e p -> v a p e"), COPY, scale=1.0 / 3.0)
-            pairs = mean_t[:].rearrange("v a p e -> v (a p e)").bitcast(F32)
-            for a in range(2):
-                nc.tensor.transpose(back[a][:, u, :], pairs[:, a * P : (a + 1) * P], ident[:])
+                    add_to_total(d, t, a, g[:, t, a * VH : (a + 1) * VH])
+            round_planes(gb[d][:], g[:])
+        g = sb("g2", [P, 2, PACK, VH], F32, "g0")
+        for a in range(2):
+            for t in range(PACK):
+                nc.vector.tensor_copy(g[:, a, t, :], h[:, t * S : (t + 1) * S].indirect(pos_t[2][:, a * VH // 16 : (a + 1) * VH // 16]))
+                add_to_total(2, t, a, g[:, a, t, :])
+            round_planes(gb[2][:, a * VH : (a + 1) * VH, :], g[:, a])
+            mean_t = sb("mean_t%d" % a, [P, 2, P, 2], BF16)
+            nc.scalar.activation(mean_t[:], total[a][:].rearrange("v (u e) p -> v u p e", e=2), COPY, scale=1.0 / 3.0)
+            pairs = mean_t[:].rearrange("v u p e -> v (u p e)").bitcast(F32)
+            for u in range(2):
+                nc.tensor.transpose(back[a][:, u, :], pairs[:, u * P : (u + 1) * P], ident[:])
         for a in range(2):
             z_pairs = z[0][:].bitcast(F32)[:, a * VH * 2 : (a + 1) * VH * 2]
             nc.scalar.copy(out=z_pairs.rearrange("p (v u) -> p v u", u=2), in_=back[a][:].rearrange("p u v -> p v u"))
 
-        flat = [gb[d][:].rearrange("p v t -> p (v t)") for d in range(2)]
+        flat = [gb[d][:].rearrange("p v t -> p (v t)") for d in range(3)]
         nc.vector.tensor_tensor(hi[:], flat[0], flat[1], MAX)
         nc.vector.tensor_tensor(lo[:], flat[0], flat[1], MIN)
-
-        def by_pairs(tile):
-            return tile[:].rearrange("p (v u e) -> p v u e", u=2, e=2)
-
-        last_v = last[:].rearrange("p u v e -> p v u e")
-        nc.vector.tensor_tensor(by_pairs(z[1]), by_pairs(hi), last_v, MAX)
-        nc.vector.tensor_tensor(by_pairs(z[2]), by_pairs(lo), last_v, MIN)
+        nc.vector.tensor_tensor(z[1][:], hi[:], flat[2], MAX)
+        nc.vector.tensor_tensor(z[2][:], lo[:], flat[2], MIN)
         zc = [sb("zc%d" % d, [P, V], U32) for d in range(3)]
         zs = [sb("zs%d" % d, [P, V], U8) for d in range(3)]
         for d in (1, 2):
@@ -224,4 +216,4 @@ def tile_picked_pna_none_p_kernel(
             cols = slice(a * VH, (a + 1) * VH)
             res = sb("res%d" % a, [P, VH], F32)
             nc.scalar.copy(out=res[:], in_=acc[a][:])
-            (nc.sync, nc.scalar)[a].dma_start(out=out[:, cols], in_=res[:])
+            nc.sync.dma_start(out=out[:, cols], in_=res[:])

@@ -19,9 +19,14 @@ MIN = mybir.AluOpType.min
 
 P = 128
 PACK = 4
+QUADS = 4
+LISTS = 3
 PASSES = K // (P * PACK)
 SH = S // 2
 VH = V // 2
+
+W1_PIECES = [(0, 0, H // 2), (0, H // 2, H), (1, 0, H // 2), (1, H // 2, 3 * H // 4), (1, 3 * H // 4, H)]
+QUANT_RUNS = [(0, 1), (1, 2), (2, PACK)]
 
 
 def tile_picked_pna_none_p_kernel(
@@ -32,37 +37,36 @@ def tile_picked_pna_none_p_kernel(
         keep = ctx.enter_context(tc.tile_pool(name="keep", bufs=1))
         psum = ctx.enter_context(tc.psum_pool(name="psum", bufs=1))
 
-        def sb(name, shape, dtype, tag=""):
-            return keep.tile(shape, dtype, name=name, tag=tag or name, align_bytes=64)
+        def sb(name, shape, dtype, bytes_of=""):
+            return keep.tile(shape, dtype, name=name, tag=bytes_of or name, align_bytes=64)
 
         def bank(b, shape):
             return psum.tile(shape, F32, name="bank%d" % b)
 
         offs_t = sb("offs_t", [P, S // 16], U16)
-        pos_t = [sb("pos_t%d" % d, [P, V // 16], U16) for d in range(3)]
+        pos_t = [sb("pos_t%d" % d, [P, V // 16], U16) for d in range(LISTS)]
         xs_all = sb("xs_all", [P, T], U8)
-        ws = sb("ws", [P, 3 * N], U8)
-        xw_all = [sb("xw_all%d" % z, [P, T], U32) for z in range(PASSES)]
-        ww = [sb("ww%d" % d, [P, N], U32) for d in range(3)]
+        ws = sb("ws", [P, LISTS * N], U8)
+        xw_all = [sb("xw_all%d" % g, [P, T], U32) for g in range(PASSES)]
+        ww = [sb("ww%d" % d, [P, N], U32) for d in range(LISTS)]
         ident = sb("ident", [P, P], F32)
 
         nc.gpsimd.memset(xs_all[:].bitcast(I32), 0)
         nc.vector.memset(ws[:].bitcast(I32), 0)
 
-        w1_rows = w1.rearrange("(z p j) c -> z p j c", z=PASSES, j=PACK)
-        chunks = [(0, 0, 256), (0, 256, 512), (1, 0, 256), (1, 256, 384), (1, 384, 512)]
-        raw = [sb("raw%d" % n, [P, PACK, c1 - c0], F32) for n, (z, c0, c1) in enumerate(chunks)]
+        w1_rows = w1.rearrange("(g p j) c -> g p j c", g=PASSES, j=PACK)
+        raw = [sb("raw%d" % n, [P, PACK, c1 - c0], F32) for n, (g, c0, c1) in enumerate(W1_PIECES)]
 
         def load_w1(n):
-            z, c0, c1 = chunks[n]
-            nc.sync.dma_start(out=raw[n][:], in_=w1_rows[z][:, :, c0:c1])
+            g, c0, c1 = W1_PIECES[n]
+            nc.sync.dma_start(out=raw[n][:], in_=w1_rows[g][:, :, c0:c1])
 
-        def load_x(z):
-            nc.sync.dma_start(out=xw_all[z][:].bitcast(I32), in_=x_words[z].rearrange("p c r -> p (c r)").bitcast(I32))
+        def load_x(g):
+            nc.sync.dma_start(out=xw_all[g][:].bitcast(I32), in_=x_words[g].rearrange("p c r -> p (c r)").bitcast(I32))
 
         load_x(0)
         nc.sync.dma_start(offs_t[:], offs)
-        for q in range(4):
+        for q in range(QUADS):
             nc.sync.dma_start(
                 out=xs_all[32 * q : 32 * q + 4 * PASSES, :].bitcast(I32), in_=x_scales[:, 4 * q : 4 * q + 4, :].bitcast(I32)
             )
@@ -70,129 +74,128 @@ def tile_picked_pna_none_p_kernel(
         load_w1(0)
         load_w1(1)
         load_x(1)
-        for n in (2, 3, 4):
+        for n in range(2, len(W1_PIECES)):
             load_w1(n)
         for d, pos in enumerate((pos1, pos2, pos3)):
             nc.sync.dma_start(pos_t[d][:], pos)
         for d, (words, scales) in enumerate(((w2_words, w2_scales), (w3_words, w3_scales), (w4_words, w4_scales))):
             nc.sync.dma_start(out=ww[d][:].bitcast(I32), in_=words[0].rearrange("p c r -> p (c r)").bitcast(I32))
-            for q in range(4):
+            for q in range(QUADS):
                 nc.sync.dma_start(
                     out=ws[32 * q : 32 * q + 4, d * N : (d + 1) * N].bitcast(I32), in_=scales[0][4 * q : 4 * q + 4, :].bitcast(I32)
                 )
 
-        w1b = [sb("w1b%d" % z, [P, PACK, P, PACK], BF16) for z in range(PASSES)]
-        w1c = [sb("w1c%d" % z, [P, H], U32) for z in range(PASSES)]
-        w1s = [sb("w1s%d" % z, [P, H], U8) for z in range(PASSES)]
+        w1b = [sb("w1b%d" % g, [P, PACK, P, PACK], BF16) for g in range(PASSES)]
+        w1c = [sb("w1c%d" % g, [P, H], U32) for g in range(PASSES)]
+        w1s = [sb("w1s%d" % g, [P, H], U8) for g in range(PASSES)]
         xs = sb("xs", [P, S], U8)
         xw = []
 
-        def cast_w1(n, m0, m1, on_vector):
-            z, c0, c1 = chunks[n]
-            src = raw[n][:].rearrange("p j (m t) -> p m j t", t=PACK)[:, m0:m1]
-            dst = w1b[z][:].rearrange("p t m j -> p m j t")[:, c0 // PACK + m0 : c0 // PACK + m1]
-            if on_vector:
-                nc.vector.tensor_copy(out=dst, in_=src)
-            else:
-                nc.scalar.copy(out=dst, in_=src)
+        def round_w1(copy, n, m_part=slice(None), t_part=slice(None)):
+            g, c0, c1 = W1_PIECES[n]
+            src = raw[n][:].rearrange("p j (m t) -> p m j t", t=PACK)
+            dst = w1b[g][:].rearrange("p t m j -> p m j t")[:, c0 // PACK : c1 // PACK]
+            copy(out=dst[:, m_part, :, t_part], in_=src[:, m_part, :, t_part])
 
-        def quant_w1(z, t0, t1):
-            nc.vector.quantize_mx(
-                out=w1c[z][:, t0 * P : t1 * P].bitcast(FP8X4),
-                scales=w1s[z][:, t0 * P : t1 * P],
-                in_=w1b[z][:, t0:t1].rearrange("p t m j -> p (t m j)"),
-            )
+        def quantise_w1(g):
+            for t0, t1 in QUANT_RUNS:
+                nc.vector.quantize_mx(
+                    out=w1c[g][:, t0 * P : t1 * P].bitcast(FP8X4),
+                    scales=w1s[g][:, t0 * P : t1 * P],
+                    in_=w1b[g][:, t0:t1].rearrange("p t m j -> p (t m j)"),
+                )
 
-        def gather_x(z, tag):
-            xw.append(sb("xw%d" % z, [P, S], U32, tag))
-            nc.vector.tensor_copy(xw[z][:], xw_all[z][:].indirect(offs_t[:]))
+        def gather_words(g, bytes_of=""):
+            xw.append(sb("xw%d" % g, [P, S], U32, bytes_of))
+            nc.vector.tensor_copy(xw[g][:], xw_all[g][:].indirect(offs_t[:]))
 
-        gather_x(0, "xw0")
+        gather_words(0)
         nc.vector.tensor_copy(xs[:], xs_all[:].indirect(offs_t[:]))
-        cast_w1(0, 0, 64, False)
-        cast_w1(1, 0, 32, False)
-        cast_w1(1, 32, 64, True)
-        quant_w1(0, 0, 1)
-        quant_w1(0, 1, 2)
-        quant_w1(0, 2, 4)
-        gather_x(1, "w1b0")
-        cast_w1(2, 0, 64, False)
-        cast_w1(3, 0, 32, True)
-        cast_w1(4, 0, 16, True)
-        cast_w1(4, 16, 32, False)
-        quant_w1(1, 0, 1)
-        quant_w1(1, 1, 2)
-        quant_w1(1, 2, 4)
+        round_w1(nc.scalar.copy, 0)
+        round_w1(nc.scalar.copy, 1, slice(0, P // 4))
+        round_w1(nc.vector.tensor_copy, 1, slice(P // 4, P // 2))
+        quantise_w1(0)
+        gather_words(1, "w1b0")
+        round_w1(nc.scalar.copy, 2)
+        round_w1(nc.vector.tensor_copy, 3)
+        round_w1(nc.vector.tensor_copy, 4, t_part=slice(0, PACK // 2))
+        round_w1(nc.scalar.copy, 4, t_part=slice(PACK // 2, PACK))
+        quantise_w1(1)
 
         hp = [[bank(2 * t + a, [P, SH]) for a in range(2)] for t in range(PACK)]
         h = sb("h", [P, PACK * S], F32)
-
-        def first_product(z, t, a):
-            nc.tensor.matmul_mx(
-                out=hp[t][a][:],
-                lhsT=w1c[z][:, t * P : (t + 1) * P].bitcast(FP8X4),
-                lhsT_scale=w1s[z][:, t * P : (t + 1) * P],
-                rhs=xw[z][:, a * SH : (a + 1) * SH].bitcast(FP8X4),
-                rhs_scale=xs[4 * z :, a * SH : (a + 1) * SH],
-                start=(z == 0),
-                stop=(z == PASSES - 1),
-            )
-
-        for z in range(PASSES):
+        for g in range(PASSES):
             for t in range(PACK):
                 for a in range(2):
-                    first_product(z, t, a)
+                    nc.tensor.matmul_mx(
+                        out=hp[t][a][:],
+                        lhsT=w1c[g][:, t * P : (t + 1) * P].bitcast(FP8X4),
+                        lhsT_scale=w1s[g][:, t * P : (t + 1) * P],
+                        rhs=xw[g][:, a * SH : (a + 1) * SH].bitcast(FP8X4),
+                        rhs_scale=xs[4 * g :, a * SH : (a + 1) * SH],
+                        start=(g == 0),
+                        stop=(g == PASSES - 1),
+                    )
         for t in range(PACK):
             for a in range(2):
-                dst = h[:, t * S + a * SH : t * S + (a + 1) * SH]
-                if (t, a) == (0, 0):
-                    nc.vector.tensor_copy(out=dst, in_=hp[t][a][:])
-                else:
-                    nc.scalar.copy(out=dst, in_=hp[t][a][:])
+                copy = nc.vector.tensor_copy if (t, a) == (0, 0) else nc.scalar.copy
+                copy(out=h[:, t * S + a * SH : t * S + (a + 1) * SH], in_=hp[t][a][:])
 
-        gb = [sb("gb%d" % d, [P, V, PACK], BF16) for d in range(3)]
+        got = [sb("g%d" % d, [P, PACK, V], F32) for d in range(LISTS)]
+        rounded = [sb("gb%d" % d, [P, V, PACK], BF16) for d in range(LISTS - 1)]
+        last = sb("last", [P, 2, V, 2], BF16)
         hi = sb("hi", [P, V * PACK], BF16)
         lo = sb("lo", [P, V * PACK], BF16)
-        z = [sb("z%d" % d, [P, V * PACK], BF16) for d in range(3)]
-        total = [bank(a, [P, PACK, P]) for a in range(2)]
+        z = [sb("z%d" % d, [P, V * PACK], BF16) for d in range(LISTS)]
+        total = [bank(u, [P, 2, 2, P]) for u in range(2)]
         back = [bank(2 + a, [P, 2, P]) for a in range(2)]
 
-        def round_planes(dst, src):
-            nc.scalar.copy(out=dst.rearrange("p (c i) t -> p c t i", i=4), in_=src.rearrange("p t (c i) -> p c t i", i=4))
-
-        def add_to_total(d, t, a, src):
-            nc.tensor.matmul(total[a][:, t, :], src, ident[:], start=((d, t) == (0, 0)), stop=((d, t) == (2, PACK - 1)), is_transpose=True)
-
-        for d in range(2):
-            g = sb("g%d" % d, [P, PACK, V], F32)
+        for d in range(LISTS):
             for t in range(PACK):
-                end = (t + 1) * S if d == 0 else PACK * S
-                nc.vector.tensor_copy(g[:, t, :], h[:, t * S : end].indirect(pos_t[d][:]))
+                end = (t + 1) * S if d == 0 or (d, t) == (1, 0) else PACK * S
+                nc.vector.tensor_copy(got[d][:, t, :], h[:, t * S : end].indirect(pos_t[d][:]))
+                u, e = divmod(t, 2)
                 for a in range(2):
-                    add_to_total(d, t, a, g[:, t, a * VH : (a + 1) * VH])
-            round_planes(gb[d][:], g[:])
-        g = sb("g2", [P, 2, PACK, VH], F32, "g0")
-        for a in range(2):
-            for t in range(PACK):
-                nc.vector.tensor_copy(g[:, a, t, :], h[:, t * S : (t + 1) * S].indirect(pos_t[2][:, a * VH // 16 : (a + 1) * VH // 16]))
-                add_to_total(2, t, a, g[:, a, t, :])
-            round_planes(gb[2][:, a * VH : (a + 1) * VH, :], g[:, a])
-            mean_t = sb("mean_t%d" % a, [P, 2, P, 2], BF16)
-            nc.scalar.activation(mean_t[:], total[a][:].rearrange("v (u e) p -> v u p e", e=2), COPY, scale=1.0 / 3.0)
-            pairs = mean_t[:].rearrange("v u p e -> v (u p e)").bitcast(F32)
-            for u in range(2):
-                nc.tensor.transpose(back[a][:, u, :], pairs[:, u * P : (u + 1) * P], ident[:])
-        for a in range(2):
-            z_pairs = z[0][:].bitcast(F32)[:, a * VH * 2 : (a + 1) * VH * 2]
-            nc.scalar.copy(out=z_pairs.rearrange("p (v u) -> p v u", u=2), in_=back[a][:].rearrange("p u v -> p v u"))
+                    nc.tensor.matmul(
+                        total[u][:, a, e, :],
+                        got[d][:, t, a * VH : (a + 1) * VH],
+                        ident[:],
+                        start=((d, e, a) == (0, 0, 0)),
+                        stop=((d, e, a) == (LISTS - 1, 1, 1)),
+                        is_transpose=True,
+                    )
+            if d < LISTS - 1:
+                nc.scalar.copy(
+                    out=rounded[d][:].rearrange("p (c i) t -> p c t i", i=4), in_=got[d][:].rearrange("p t (c i) -> p c t i", i=4)
+                )
 
-        flat = [gb[d][:].rearrange("p v t -> p (v t)") for d in range(3)]
+        for u in range(2):
+            nc.scalar.copy(
+                out=last[:, u].rearrange("p (c i) e -> p c e i", i=4),
+                in_=got[LISTS - 1][:, 2 * u : 2 * u + 2, :].rearrange("p e (c i) -> p c e i", i=4),
+            )
+            mean_t = sb("mean_t%d" % u, [P, 2, P, 2], BF16)
+            nc.scalar.activation(mean_t[:], total[u][:].rearrange("v a e p -> v a p e"), COPY, scale=1.0 / LISTS)
+            pairs = mean_t[:].rearrange("v a p e -> v (a p e)").bitcast(F32)
+            for a in range(2):
+                nc.tensor.transpose(back[a][:, u, :], pairs[:, a * P : (a + 1) * P], ident[:])
+        for a in range(2):
+            mean_words = z[0][:].bitcast(F32)[:, a * VH * 2 : (a + 1) * VH * 2]
+            nc.scalar.copy(out=mean_words.rearrange("p (v u) -> p v u", u=2), in_=back[a][:].rearrange("p u v -> p v u"))
+
+        flat = [rounded[d][:].rearrange("p v t -> p (v t)") for d in range(LISTS - 1)]
         nc.vector.tensor_tensor(hi[:], flat[0], flat[1], MAX)
         nc.vector.tensor_tensor(lo[:], flat[0], flat[1], MIN)
-        nc.vector.tensor_tensor(z[1][:], hi[:], flat[2], MAX)
-        nc.vector.tensor_tensor(z[2][:], lo[:], flat[2], MIN)
-        zc = [sb("zc%d" % d, [P, V], U32) for d in range(3)]
-        zs = [sb("zs%d" % d, [P, V], U8) for d in range(3)]
+
+        def by_pairs(tile):
+            return tile[:].rearrange("p (v u e) -> p v u e", u=2, e=2)
+
+        last_v = last[:].rearrange("p u v e -> p v u e")
+        nc.vector.tensor_tensor(by_pairs(z[1]), by_pairs(hi), last_v, MAX)
+        nc.vector.tensor_tensor(by_pairs(z[2]), by_pairs(lo), last_v, MIN)
+
+        zc = [sb("zc%d" % d, [P, V], U32) for d in range(LISTS)]
+        zs = [sb("zs%d" % d, [P, V], U8) for d in range(LISTS)]
         for d in (1, 2):
             nc.vector.quantize_mx(out=zc[d][:].bitcast(FP8X4), scales=zs[d][:], in_=z[d][:])
         for a in range(2):
@@ -210,10 +213,9 @@ def tile_picked_pna_none_p_kernel(
                     rhs=zc[d][:, cols].bitcast(FP8X4),
                     rhs_scale=zs[d][:, cols],
                     start=(n == 0),
-                    stop=(n == 2),
+                    stop=(n == LISTS - 1),
                 )
         for a in range(2):
-            cols = slice(a * VH, (a + 1) * VH)
             res = sb("res%d" % a, [P, VH], F32)
             nc.scalar.copy(out=res[:], in_=acc[a][:])
-            nc.sync.dma_start(out=out[:, cols], in_=res[:])
+            nc.sync.dma_start(out=out[:, a * VH : (a + 1) * VH], in_=res[:])

@@ -123,7 +123,7 @@ def tile_picked_pna_none_p_kernel(
         quantise_w1(1)
 
         hp = [[bank(2 * t + a, [P, SH]) for a in range(2)] for t in range(PACK)]
-        h = sb("h", [P, PACK * S], F32)
+        h = [sb("h%d" % t, [P, S], F32) for t in range(PACK)]
         for g in range(PASSES):
             for t in range(PACK):
                 for a in range(2):
@@ -139,60 +139,71 @@ def tile_picked_pna_none_p_kernel(
         for t in range(PACK):
             for a in range(2):
                 copy = nc.vector.tensor_copy if (t, a) == (0, 0) else nc.scalar.copy
-                copy(out=h[:, t * S + a * SH : t * S + (a + 1) * SH], in_=hp[t][a][:])
+                copy(out=h[t][:, a * SH : (a + 1) * SH], in_=hp[t][a][:])
 
-        got = [sb("g%d" % d, [P, PACK, V], F32) for d in range(LISTS)]
-        rounded = [sb("gb%d" % d, [P, V, PACK], BF16) for d in range(LISTS - 1)]
+        got = [sb("g%d" % u, [P, LISTS, 2, V], F32) for u in range(2)]
         last = sb("last", [P, 2, V, 2], BF16)
-        hi = sb("hi", [P, V * PACK], BF16)
-        lo = sb("lo", [P, V * PACK], BF16)
+        hi = sb("hi", [P, 2, V * 2], BF16)
+        lo = sb("lo", [P, 2, V * 2], BF16)
         z = [sb("z%d" % d, [P, V * PACK], BF16) for d in range(LISTS)]
         total = [bank(u, [P, 2, 2, P]) for u in range(2)]
         back = [bank(2 + a, [P, 2, P]) for a in range(2)]
 
-        for d in range(LISTS):
-            for t in range(PACK):
-                end = (t + 1) * S if d == 0 or (d, t) == (1, 0) else PACK * S
-                nc.vector.tensor_copy(got[d][:, t, :], h[:, t * S : end].indirect(pos_t[d][:]))
-                u, e = divmod(t, 2)
-                for a in range(2):
-                    nc.tensor.matmul(
-                        total[u][:, a, e, :],
-                        got[d][:, t, a * VH : (a + 1) * VH],
-                        ident[:],
-                        start=((d, e, a) == (0, 0, 0)),
-                        stop=((d, e, a) == (LISTS - 1, 1, 1)),
-                        is_transpose=True,
-                    )
-            if d < LISTS - 1:
-                nc.scalar.copy(
-                    out=rounded[d][:].rearrange("p (c i) t -> p c t i", i=4), in_=got[d][:].rearrange("p t (c i) -> p c t i", i=4)
+        def gather(d, t, on_vector, first, final):
+            u, e = divmod(t, 2)
+            window = h[t][:].indirect(pos_t[d][:])
+            if on_vector:
+                nc.vector.tensor_copy(got[u][:, d, e, :], window)
+            else:
+                nc.scalar.activation(got[u][:, d, e, :], window, COPY)
+            for a in range(2):
+                nc.tensor.matmul(
+                    total[u][:, a, e, :],
+                    got[u][:, d, e, a * VH : (a + 1) * VH],
+                    ident[:],
+                    start=(first and a == 0),
+                    stop=(final and a == 1),
+                    is_transpose=True,
                 )
 
-        for u in range(2):
-            nc.scalar.copy(
+        def round_last(u):
+            nc.vector.tensor_copy(
                 out=last[:, u].rearrange("p (c i) e -> p c e i", i=4),
-                in_=got[LISTS - 1][:, 2 * u : 2 * u + 2, :].rearrange("p e (c i) -> p c e i", i=4),
+                in_=got[u][:, LISTS - 1].rearrange("p e (c i) -> p c e i", i=4),
             )
+
+        def compare_first_two(u):
+            first, second = (got[u][:, d].rearrange("p e (c i) -> p c e i", i=4) for d in range(2))
+            nc.vector.tensor_tensor(hi[:, u].rearrange("p (c i e) -> p c e i", i=4, e=2), first, second, MAX)
+            nc.vector.tensor_tensor(lo[:, u].rearrange("p (c i e) -> p c e i", i=4, e=2), first, second, MIN)
+
+        def mean_out(u):
             mean_t = sb("mean_t%d" % u, [P, 2, P, 2], BF16)
             nc.scalar.activation(mean_t[:], total[u][:].rearrange("v a e p -> v a p e"), COPY, scale=1.0 / LISTS)
             pairs = mean_t[:].rearrange("v a p e -> v (a p e)").bitcast(F32)
             for a in range(2):
                 nc.tensor.transpose(back[a][:, u, :], pairs[:, a * P : (a + 1) * P], ident[:])
+
+        ORDER = [[(0, 0, 1), (1, 0, 1), (2, 0, 1), (0, 1, 1), (1, 1, 0), (2, 1, 0)],
+                 [(0, 3, 1), (0, 2, 0), (1, 3, 1), (1, 2, 0), (2, 2, 0), (2, 3, 0)]]
+        for u in range(2):
+            for n, (d, t, on_vector) in enumerate(ORDER[u]):
+                gather(d, t, on_vector, n == 0, n == 5)
+        for u in range(2):
+            compare_first_two(u)
+            round_last(u)
+        for u in range(2):
+            mean_out(u)
         for a in range(2):
             mean_words = z[0][:].bitcast(F32)[:, a * VH * 2 : (a + 1) * VH * 2]
             nc.scalar.copy(out=mean_words.rearrange("p (v u) -> p v u", u=2), in_=back[a][:].rearrange("p u v -> p v u"))
 
-        flat = [rounded[d][:].rearrange("p v t -> p (v t)") for d in range(LISTS - 1)]
-        nc.vector.tensor_tensor(hi[:], flat[0], flat[1], MAX)
-        nc.vector.tensor_tensor(lo[:], flat[0], flat[1], MIN)
-
-        def by_pairs(tile):
-            return tile[:].rearrange("p (v u e) -> p v u e", u=2, e=2)
+        def by_target(pairs):
+            return pairs.rearrange("p u (v e) -> p v u e", e=2)
 
         last_v = last[:].rearrange("p u v e -> p v u e")
-        nc.vector.tensor_tensor(by_pairs(z[1]), by_pairs(hi), last_v, MAX)
-        nc.vector.tensor_tensor(by_pairs(z[2]), by_pairs(lo), last_v, MIN)
+        nc.vector.tensor_tensor(z[1][:].rearrange("p (v u e) -> p v u e", u=2, e=2), by_target(hi[:]), last_v, MAX)
+        nc.vector.tensor_tensor(z[2][:].rearrange("p (v u e) -> p v u e", u=2, e=2), by_target(lo[:]), last_v, MIN)
 
         zc = [sb("zc%d" % d, [P, V], U32) for d in range(LISTS)]
         zs = [sb("zs%d" % d, [P, V], U8) for d in range(LISTS)]

@@ -122,47 +122,47 @@ def tile_picked_pna_none_p_kernel(
         round_w1(nc.scalar.copy, 4, t_part=slice(PACK // 2, PACK))
         quantise_w1(1)
 
-        hp = [[bank(2 * t + a, [P, SH]) for a in range(2)] for t in range(PACK)]
+        groups = [(0, 0, SH), (0, SH, S)] + [(t, 0, S) for t in range(1, PACK)]
+        hp = [bank(b, [P, s1 - s0]) for b, (t, s0, s1) in enumerate(groups)]
         h = [sb("h%d" % t, [P, S], F32) for t in range(PACK)]
         for g in range(PASSES):
-            for t in range(PACK):
-                for a in range(2):
-                    nc.tensor.matmul_mx(
-                        out=hp[t][a][:],
-                        lhsT=w1c[g][:, t * P : (t + 1) * P].bitcast(FP8X4),
-                        lhsT_scale=w1s[g][:, t * P : (t + 1) * P],
-                        rhs=xw[g][:, a * SH : (a + 1) * SH].bitcast(FP8X4),
-                        rhs_scale=xs[4 * g :, a * SH : (a + 1) * SH],
-                        start=(g == 0),
-                        stop=(g == PASSES - 1),
-                    )
-        for t in range(PACK):
-            for a in range(2):
-                copy = nc.vector.tensor_copy if (t, a) == (0, 0) else nc.scalar.copy
-                copy(out=h[t][:, a * SH : (a + 1) * SH], in_=hp[t][a][:])
+            for b, (t, s0, s1) in enumerate(groups):
+                nc.tensor.matmul_mx(
+                    out=hp[b][:],
+                    lhsT=w1c[g][:, t * P : (t + 1) * P].bitcast(FP8X4),
+                    lhsT_scale=w1s[g][:, t * P : (t + 1) * P],
+                    rhs=xw[g][:, s0:s1].bitcast(FP8X4),
+                    rhs_scale=xs[4 * g :, s0:s1],
+                    start=(g == 0),
+                    stop=(g == PASSES - 1),
+                )
+        for b, (t, s0, s1) in enumerate(groups):
+            copy = nc.vector.tensor_copy if b == 0 else nc.scalar.copy
+            copy(out=h[t][:, s0:s1], in_=hp[b][:])
 
         got = [sb("g%d" % u, [P, LISTS, 2, V], F32) for u in range(2)]
         last = sb("last", [P, 2, V, 2], BF16)
         hi = sb("hi", [P, 2, V * 2], BF16)
         lo = sb("lo", [P, 2, V * 2], BF16)
         z = [sb("z%d" % d, [P, V * PACK], BF16) for d in range(LISTS)]
-        total = [bank(u, [P, 2, 2, P]) for u in range(2)]
-        back = [bank(2 + a, [P, 2, P]) for a in range(2)]
+        total = [bank(5 + u, [P, 2, 2, P]) for u in range(2)]
+        back = [bank(a, [P, 2, P]) for a in range(2)]
 
-        def gather(d, t, on_vector, first, final):
+        def gather(d, t, a0, a1, on_vector, first, final):
             u, e = divmod(t, 2)
-            window = h[t][:].indirect(pos_t[d][:])
+            window = h[t][:].indirect(pos_t[d][:, a0 * VH // 16 : a1 * VH // 16])
+            into = got[u][:, d, e, a0 * VH : a1 * VH]
             if on_vector:
-                nc.vector.tensor_copy(got[u][:, d, e, :], window)
+                nc.vector.tensor_copy(into, window)
             else:
-                nc.scalar.activation(got[u][:, d, e, :], window, COPY)
-            for a in range(2):
+                nc.scalar.activation(into, window, COPY)
+            for a in range(a0, a1):
                 nc.tensor.matmul(
                     total[u][:, a, e, :],
                     got[u][:, d, e, a * VH : (a + 1) * VH],
                     ident[:],
-                    start=(first and a == 0),
-                    stop=(final and a == 1),
+                    start=(first and a == a0),
+                    stop=(final and a == a1 - 1),
                     is_transpose=True,
                 )
 
@@ -177,23 +177,24 @@ def tile_picked_pna_none_p_kernel(
             nc.vector.tensor_tensor(hi[:, u].rearrange("p (c i e) -> p c e i", i=4, e=2), first, second, MAX)
             nc.vector.tensor_tensor(lo[:, u].rearrange("p (c i e) -> p c e i", i=4, e=2), first, second, MIN)
 
-        def mean_out(u):
-            mean_t = sb("mean_t%d" % u, [P, 2, P, 2], BF16)
-            nc.scalar.activation(mean_t[:], total[u][:].rearrange("v a e p -> v a p e"), COPY, scale=1.0 / LISTS)
+        def mean_out(u, a0, a1):
+            mean_t = sb("mean_t%d%d" % (u, a0), [P, a1 - a0, P, 2], BF16)
+            nc.scalar.activation(mean_t[:], total[u][:, a0:a1].rearrange("v a e p -> v a p e"), COPY, scale=1.0 / LISTS)
             pairs = mean_t[:].rearrange("v a p e -> v (a p e)").bitcast(F32)
-            for a in range(2):
-                nc.tensor.transpose(back[a][:, u, :], pairs[:, a * P : (a + 1) * P], ident[:])
+            for a in range(a0, a1):
+                nc.tensor.transpose(back[a][:, u, :], pairs[:, (a - a0) * P : (a - a0 + 1) * P], ident[:])
 
-        ORDER = [[(0, 0, 1), (1, 0, 1), (2, 0, 1), (0, 1, 1), (1, 1, 0), (2, 1, 0)],
-                 [(0, 3, 1), (0, 2, 0), (1, 3, 1), (1, 2, 0), (2, 2, 0), (2, 3, 0)]]
+        ORDER = [[(0, 0, 0, 2, 1), (1, 0, 0, 2, 1), (2, 0, 0, 2, 1), (0, 1, 0, 2, 1), (1, 1, 0, 2, 0), (2, 1, 0, 2, 0)],
+                 [(0, 3, 0, 2, 1), (0, 2, 0, 2, 0), (1, 3, 0, 1, 1), (1, 2, 0, 2, 0), (1, 3, 1, 2, 0), (2, 2, 0, 2, 0), (2, 3, 0, 2, 0)]]
         for u in range(2):
-            for n, (d, t, on_vector) in enumerate(ORDER[u]):
-                gather(d, t, on_vector, n == 0, n == 5)
+            for n, (d, t, a0, a1, on_vector) in enumerate(ORDER[u]):
+                gather(d, t, a0, a1, on_vector, n == 0, n == len(ORDER[u]) - 1)
         for u in range(2):
             compare_first_two(u)
             round_last(u)
-        for u in range(2):
-            mean_out(u)
+        mean_out(0, 0, 2)
+        mean_out(1, 0, 1)
+        mean_out(1, 1, 2)
         for a in range(2):
             mean_words = z[0][:].bitcast(F32)[:, a * VH * 2 : (a + 1) * VH * 2]
             nc.scalar.copy(out=mean_words.rearrange("p (v u) -> p v u", u=2), in_=back[a][:].rearrange("p u v -> p v u"))
@@ -213,7 +214,7 @@ def tile_picked_pna_none_p_kernel(
             cols = slice(a * VH, (a + 1) * VH)
             nc.vector.quantize_mx(out=zc[0][:, cols].bitcast(FP8X4), scales=zs[0][:, cols], in_=z[0][:, a * VH * PACK : (a + 1) * VH * PACK])
 
-        acc = [bank(4 + a, [P, VH]) for a in range(2)]
+        acc = [bank(2 + a, [P, VH]) for a in range(2)]
         for n, d in enumerate((1, 2, 0)):
             for a in range(2):
                 cols = slice(a * VH, (a + 1) * VH)

@@ -16,6 +16,8 @@ FP8X4 = mybir.dt.float8_e4m3fn_x4
 COPY = mybir.ActivationFunctionType.Copy
 MAX = mybir.AluOpType.max
 MIN = mybir.AluOpType.min
+MULT = mybir.AluOpType.mult
+ADD = mybir.AluOpType.add
 
 P = 128
 PACK = 4
@@ -148,34 +150,37 @@ def tile_picked_pna_none_p_kernel(
         total = [bank(5 + u, [P, 2, 2, P]) for u in range(2)]
         back = [bank(a, [P, 2, P]) for a in range(2)]
 
-        def gather(d, t, a0, a1, on_vector, first, final):
+        def gather(d, t, v0, v1, on_vector):
             u, e = divmod(t, 2)
-            window = h[t][:].indirect(pos_t[d][:, a0 * VH // 16 : a1 * VH // 16])
-            into = got[u][:, d, e, a0 * VH : a1 * VH]
+            window = h[t][:].indirect(pos_t[d][:, v0 // 16 : v1 // 16])
             if on_vector:
-                nc.vector.tensor_copy(into, window)
+                nc.vector.tensor_copy(got[u][:, d, e, v0:v1], window)
             else:
-                nc.scalar.activation(into, window, COPY)
-            for a in range(a0, a1):
+                nc.scalar.activation(got[u][:, d, e, v0:v1], window, COPY)
+
+        def add_up(d, t, first, final):
+            u, e = divmod(t, 2)
+            for a in range(2):
                 nc.tensor.matmul(
                     total[u][:, a, e, :],
                     got[u][:, d, e, a * VH : (a + 1) * VH],
                     ident[:],
-                    start=(first and a == a0),
-                    stop=(final and a == a1 - 1),
+                    start=(first and a == 0),
+                    stop=(final and a == 1),
                     is_transpose=True,
                 )
 
         def round_last(u):
-            nc.vector.tensor_copy(
-                out=last[:, u].rearrange("p (c i) e -> p c e i", i=4),
-                in_=got[u][:, LISTS - 1].rearrange("p e (c i) -> p c e i", i=4),
-            )
+            dst = last[:, u].rearrange("p (c i) e -> p c e i", i=4)
+            src = got[u][:, LISTS - 1].rearrange("p e (c i) -> p c e i", i=4)
+            if u == 0:
+                nc.gpsimd.tensor_scalar(dst, src, 1.0, 0.0, MULT, ADD)
+            else:
+                nc.vector.tensor_copy(out=dst, in_=src)
 
-        def compare_first_two(u):
+        def compare_first_two(into, u, op):
             first, second = (got[u][:, d].rearrange("p e (c i) -> p c e i", i=4) for d in range(2))
-            nc.vector.tensor_tensor(hi[:, u].rearrange("p (c i e) -> p c e i", i=4, e=2), first, second, MAX)
-            nc.vector.tensor_tensor(lo[:, u].rearrange("p (c i e) -> p c e i", i=4, e=2), first, second, MIN)
+            nc.vector.tensor_tensor(into[:, u].rearrange("p (c i e) -> p c e i", i=4, e=2), first, second, op)
 
         def mean_out(u, a0, a1):
             mean_t = sb("mean_t%d%d" % (u, a0), [P, a1 - a0, P, 2], BF16)
@@ -184,13 +189,18 @@ def tile_picked_pna_none_p_kernel(
             for a in range(a0, a1):
                 nc.tensor.transpose(back[a][:, u, :], pairs[:, (a - a0) * P : (a - a0 + 1) * P], ident[:])
 
-        ORDER = [[(0, 0, 0, 2, 1), (1, 0, 0, 2, 1), (2, 0, 0, 2, 1), (0, 1, 0, 2, 1), (1, 1, 0, 2, 0), (2, 1, 0, 2, 0)],
-                 [(0, 3, 0, 2, 1), (0, 2, 0, 2, 0), (1, 3, 0, 1, 1), (1, 2, 0, 2, 0), (1, 3, 1, 2, 0), (2, 2, 0, 2, 0), (2, 3, 0, 2, 0)]]
+        ORDER = [[(0, 0, V), (1, 0, V), (2, 0, V), (0, 1, V), (2, 1, 0), (1, 1, 0)],
+                 [(0, 3, V), (0, 2, 0), (1, 2, 0), (1, 3, V // 2), (2, 2, 0), (2, 3, 0)]]
         for u in range(2):
-            for n, (d, t, a0, a1, on_vector) in enumerate(ORDER[u]):
-                gather(d, t, a0, a1, on_vector, n == 0, n == len(ORDER[u]) - 1)
+            for n, (d, t, split) in enumerate(ORDER[u]):
+                if split > 0:
+                    gather(d, t, 0, split, True)
+                if split < V:
+                    gather(d, t, split, V, False)
+                add_up(d, t, n == 0, n == len(ORDER[u]) - 1)
         for u in range(2):
-            compare_first_two(u)
+            compare_first_two(hi, u, MAX)
+            compare_first_two(lo, u, MIN)
             round_last(u)
         mean_out(0, 0, 2)
         mean_out(1, 0, 1)

from contextlib import ExitStack

import concourse.mybir as mybir
from concourse.masks import make_identity

K, T, S, V, H, N = 1024, 1024, 512, 256, 512, 128
FLOPS = 2 * K * H * S + 3 * 2 * H * N * V

F32 = mybir.dt.float32
BF16 = mybir.dt.bfloat16
I32 = mybir.dt.int32
U32 = mybir.dt.uint32
U16 = mybir.dt.uint16
U8 = mybir.dt.uint8
FP8X4 = mybir.dt.float8_e4m3fn_x4
COPY = mybir.ActivationFunctionType.Copy
MAX = mybir.AluOpType.max
MIN = mybir.AluOpType.min
MULT = mybir.AluOpType.mult
ADD = mybir.AluOpType.add

P = 128
PACK = 4
QUADS = 4
LISTS = 3
PASSES = K // (P * PACK)
SH = S // 2
VH = V // 2

W1_PIECES = [(0, 0, H // 2), (0, H // 2, H), (1, 0, H // 2), (1, H // 2, 3 * H // 4), (1, 3 * H // 4, H)]
QUANT_RUNS = [(0, 1), (1, 2), (2, PACK)]


def tile_picked_pna_none_p_kernel(
    tc, x_words, x_scales, w1, w2_words, w2_scales, w3_words, w3_scales, w4_words, w4_scales, offs, pos1, pos2, pos3, out
):
    nc = tc.nc
    with ExitStack() as ctx:
        keep = ctx.enter_context(tc.tile_pool(name="keep", bufs=1))
        psum = ctx.enter_context(tc.psum_pool(name="psum", bufs=1))

        def sb(name, shape, dtype, bytes_of=""):
            return keep.tile(shape, dtype, name=name, tag=bytes_of or name, align_bytes=64)

        def bank(b, shape):
            return psum.tile(shape, F32, name="bank%d" % b)

        offs_t = sb("offs_t", [P, S // 16], U16)
        pos_t = [sb("pos_t%d" % d, [P, V // 16], U16) for d in range(LISTS)]
        xs_all = sb("xs_all", [P, T], U8)
        ws = sb("ws", [P, LISTS * N], U8)
        xw_all = [sb("xw_all%d" % g, [P, T], U32) for g in range(PASSES)]
        ww = [sb("ww%d" % d, [P, N], U32) for d in range(LISTS)]
        ident = sb("ident", [P, P], F32)

        nc.gpsimd.memset(xs_all[:].bitcast(I32), 0)
        nc.vector.memset(ws[:].bitcast(I32), 0)

        w1_rows = w1.rearrange("(g p j) c -> g p j c", g=PASSES, j=PACK)
        raw = [sb("raw%d" % n, [P, PACK, c1 - c0], F32) for n, (g, c0, c1) in enumerate(W1_PIECES)]

        def load_w1(n):
            g, c0, c1 = W1_PIECES[n]
            nc.sync.dma_start(out=raw[n][:], in_=w1_rows[g][:, :, c0:c1])

        def load_x(g):
            nc.sync.dma_start(out=xw_all[g][:].bitcast(I32), in_=x_words[g].rearrange("p c r -> p (c r)").bitcast(I32))

        load_x(0)
        nc.sync.dma_start(offs_t[:], offs)
        for q in range(QUADS):
            nc.sync.dma_start(
                out=xs_all[32 * q : 32 * q + 4 * PASSES, :].bitcast(I32), in_=x_scales[:, 4 * q : 4 * q + 4, :].bitcast(I32)
            )
        make_identity(nc, ident[:])
        load_w1(0)
        load_w1(1)
        load_x(1)
        for n in range(2, len(W1_PIECES)):
            load_w1(n)
        for d, pos in enumerate((pos1, pos2, pos3)):
            nc.sync.dma_start(pos_t[d][:], pos)
        for d, (words, scales) in enumerate(((w2_words, w2_scales), (w3_words, w3_scales), (w4_words, w4_scales))):
            nc.sync.dma_start(out=ww[d][:].bitcast(I32), in_=words[0].rearrange("p c r -> p (c r)").bitcast(I32))
            for q in range(QUADS):
                nc.sync.dma_start(
                    out=ws[32 * q : 32 * q + 4, d * N : (d + 1) * N].bitcast(I32), in_=scales[0][4 * q : 4 * q + 4, :].bitcast(I32)
                )

        w1b = [sb("w1b%d" % g, [P, PACK, P, PACK], BF16) for g in range(PASSES)]
        w1c = [sb("w1c%d" % g, [P, H], U32) for g in range(PASSES)]
        w1s = [sb("w1s%d" % g, [P, H], U8) for g in range(PASSES)]
        xs = sb("xs", [P, S], U8)
        xw = []

        def round_w1(copy, n, m_part=slice(None), t_part=slice(None)):
            g, c0, c1 = W1_PIECES[n]
            src = raw[n][:].rearrange("p j (m t) -> p m j t", t=PACK)
            dst = w1b[g][:].rearrange("p t m j -> p m j t")[:, c0 // PACK : c1 // PACK]
            copy(out=dst[:, m_part, :, t_part], in_=src[:, m_part, :, t_part])

        def quantise_w1(g):
            for t0, t1 in QUANT_RUNS:
                nc.vector.quantize_mx(
                    out=w1c[g][:, t0 * P : t1 * P].bitcast(FP8X4),
                    scales=w1s[g][:, t0 * P : t1 * P],
                    in_=w1b[g][:, t0:t1].rearrange("p t m j -> p (t m j)"),
                )

        def gather_words(g, bytes_of=""):
            xw.append(sb("xw%d" % g, [P, S], U32, bytes_of))
            nc.vector.tensor_copy(xw[g][:], xw_all[g][:].indirect(offs_t[:]))

        gather_words(0)
        nc.vector.tensor_copy(xs[:], xs_all[:].indirect(offs_t[:]))
        round_w1(nc.scalar.copy, 0)
        round_w1(nc.scalar.copy, 1, slice(0, P // 4))
        round_w1(nc.vector.tensor_copy, 1, slice(P // 4, P // 2))
        quantise_w1(0)
        gather_words(1, "w1b0")
        round_w1(nc.scalar.copy, 2)
        round_w1(nc.vector.tensor_copy, 3)
        round_w1(nc.vector.tensor_copy, 4, t_part=slice(0, PACK // 2))
        round_w1(nc.scalar.copy, 4, t_part=slice(PACK // 2, PACK))
        quantise_w1(1)

        groups = [(0, 0, SH), (0, SH, S)] + [(t, 0, S) for t in range(1, PACK)]
        hp = [bank(b, [P, s1 - s0]) for b, (t, s0, s1) in enumerate(groups)]
        h = [sb("h%d" % t, [P, S], F32) for t in range(PACK)]
        for g in range(PASSES):
            for b, (t, s0, s1) in enumerate(groups):
                nc.tensor.matmul_mx(
                    out=hp[b][:],
                    lhsT=w1c[g][:, t * P : (t + 1) * P].bitcast(FP8X4),
                    lhsT_scale=w1s[g][:, t * P : (t + 1) * P],
                    rhs=xw[g][:, s0:s1].bitcast(FP8X4),
                    rhs_scale=xs[4 * g :, s0:s1],
                    start=(g == 0),
                    stop=(g == PASSES - 1),
                )
        for b, (t, s0, s1) in enumerate(groups):
            copy = nc.vector.tensor_copy if b == 0 else nc.scalar.copy
            copy(out=h[t][:, s0:s1], in_=hp[b][:])

        got = [sb("g%d" % u, [P, LISTS, 2, V], F32) for u in range(2)]
        last = sb("last", [P, 2, V, 2], BF16)
        hi = sb("hi", [P, 2, V * 2], BF16)
        lo = sb("lo", [P, 2, V * 2], BF16)
        z = [sb("z%d" % d, [P, V * PACK], BF16) for d in range(LISTS)]
        total = [bank(5 + u, [P, 2, 2, P]) for u in range(2)]
        back = [bank(a, [P, 2, P]) for a in range(2)]

        def gather(d, t, v0, v1, on_vector):
            u, e = divmod(t, 2)
            window = h[t][:].indirect(pos_t[d][:, v0 // 16 : v1 // 16])
            if on_vector:
                nc.vector.tensor_copy(got[u][:, d, e, v0:v1], window)
            else:
                nc.scalar.activation(got[u][:, d, e, v0:v1], window, COPY)

        def add_up(d, t, first, final):
            u, e = divmod(t, 2)
            for a in range(2):
                nc.tensor.matmul(
                    total[u][:, a, e, :],
                    got[u][:, d, e, a * VH : (a + 1) * VH],
                    ident[:],
                    start=(first and a == 0),
                    stop=(final and a == 1),
                    is_transpose=True,
                )

        def round_last(u):
            dst = last[:, u].rearrange("p (c i) e -> p c e i", i=4)
            src = got[u][:, LISTS - 1].rearrange("p e (c i) -> p c e i", i=4)
            if u == 0:
                nc.gpsimd.tensor_scalar(dst, src, 1.0, 0.0, MULT, ADD)
            else:
                nc.vector.tensor_copy(out=dst, in_=src)

        def compare_first_two(into, u, op):
            first, second = (got[u][:, d].rearrange("p e (c i) -> p c e i", i=4) for d in range(2))
            nc.vector.tensor_tensor(into[:, u].rearrange("p (c i e) -> p c e i", i=4, e=2), first, second, op)

        def mean_out(u, a0, a1):
            mean_t = sb("mean_t%d%d" % (u, a0), [P, a1 - a0, P, 2], BF16)
            nc.scalar.activation(mean_t[:], total[u][:, a0:a1].rearrange("v a e p -> v a p e"), COPY, scale=1.0 / LISTS)
            pairs = mean_t[:].rearrange("v a p e -> v (a p e)").bitcast(F32)
            for a in range(a0, a1):
                nc.tensor.transpose(back[a][:, u, :], pairs[:, (a - a0) * P : (a - a0 + 1) * P], ident[:])

        ORDER = [[(0, 0, V), (1, 0, V), (2, 0, V), (0, 1, V), (2, 1, 0), (1, 1, 0)],
                 [(0, 3, V), (0, 2, 0), (1, 2, 0), (1, 3, V // 2), (2, 2, 0), (2, 3, 0)]]
        for u in range(2):
            for n, (d, t, split) in enumerate(ORDER[u]):
                if split > 0:
                    gather(d, t, 0, split, True)
                if split < V:
                    gather(d, t, split, V, False)
                add_up(d, t, n == 0, n == len(ORDER[u]) - 1)
        for u in range(2):
            compare_first_two(hi, u, MAX)
            compare_first_two(lo, u, MIN)
            round_last(u)
        mean_out(0, 0, 2)
        mean_out(1, 0, 1)
        mean_out(1, 1, 2)
        for a in range(2):
            mean_words = z[0][:].bitcast(F32)[:, a * VH * 2 : (a + 1) * VH * 2]
            nc.scalar.copy(out=mean_words.rearrange("p (v u) -> p v u", u=2), in_=back[a][:].rearrange("p u v -> p v u"))

        def by_target(pairs):
            return pairs.rearrange("p u (v e) -> p v u e", e=2)

        last_v = last[:].rearrange("p u v e -> p v u e")
        nc.vector.tensor_tensor(z[1][:].rearrange("p (v u e) -> p v u e", u=2, e=2), by_target(hi[:]), last_v, MAX)
        nc.vector.tensor_tensor(z[2][:].rearrange("p (v u e) -> p v u e", u=2, e=2), by_target(lo[:]), last_v, MIN)

        zc = [sb("zc%d" % d, [P, V], U32) for d in range(LISTS)]
        zs = [sb("zs%d" % d, [P, V], U8) for d in range(LISTS)]
        for d in (1, 2):
            nc.vector.quantize_mx(out=zc[d][:].bitcast(FP8X4), scales=zs[d][:], in_=z[d][:])
        for a in range(2):
            cols = slice(a * VH, (a + 1) * VH)
            nc.vector.quantize_mx(out=zc[0][:, cols].bitcast(FP8X4), scales=zs[0][:, cols], in_=z[0][:, a * VH * PACK : (a + 1) * VH * PACK])

        acc = [bank(2 + a, [P, VH]) for a in range(2)]
        for n, d in enumerate((1, 2, 0)):
            for a in range(2):
                cols = slice(a * VH, (a + 1) * VH)
                nc.tensor.matmul_mx(
                    out=acc[a][:],
                    lhsT=ww[d][:].bitcast(FP8X4),
                    lhsT_scale=ws[:, d * N : (d + 1) * N],
                    rhs=zc[d][:, cols].bitcast(FP8X4),
                    rhs_scale=zs[d][:, cols],
                    start=(n == 0),
                    stop=(n == LISTS - 1),
                )
        for a in range(2):
            res = sb("res%d" % a, [P, VH], F32)
            nc.scalar.copy(out=res[:], in_=acc[a][:])
            nc.sync.dma_start(out=out[:, a * VH : (a + 1) * VH], in_=res[:])
